import numpy as np
import ml_dtypes


def mxq(x, axis, fmt="e4m3"):
    dtype, down = {"e4m3": (ml_dtypes.float8_e4m3fn, 7), "e5m2": (ml_dtypes.float8_e5m2, 14)}[fmt]
    v = np.moveaxis(np.asarray(x, np.float32).astype(ml_dtypes.bfloat16).astype(np.float64), axis, -1)
    blocks = v.reshape(v.shape[:-1] + (-1, 32))
    amax = np.abs(blocks).max(-1, keepdims=True)
    byte = np.maximum(np.where(amax > 0, np.frexp(amax)[1] - 1 + 127, 0) - down, 1)
    scale = np.exp2(byte - 127.0)
    codes = (blocks / scale).astype(np.float32).astype(dtype).astype(np.float64)
    return np.moveaxis((codes * scale).reshape(v.shape), -1, axis)


WIDE = False


def mx_kscale(k):
    if not WIDE:
        return np.ones(k)
    levels = np.array([10, -10, 5, -5, 0])
    if k % 512:
        return np.exp2(np.random.permutation(np.resize(levels, k // 32))).repeat(32)
    a = np.empty((k // 512, 16))
    for p in range(k // 512):
        a[p, :8] = np.random.permutation(np.resize(levels, 8))
        for g in range(8):
            far = levels[np.abs(levels - a[p, g]) >= 10]
            a[p, g + 8] = far[np.random.randint(len(far))]
    return np.exp2(a.ravel()).repeat(32)


def f64(x):
    return np.asarray(x).astype(np.float64)


def striped(idx):
    return np.tile(idx.reshape(-1, 16).T, (8, 1)).astype(np.uint16)


def unstriped(offs):
    return offs[:16].T.reshape(-1).astype(np.int64)


E2M1 = np.array([0.0, 0.5, 1.0, 1.5, 2.0, 3.0, 4.0, 6.0, -0.0, -0.5, -1.0, -1.5, -2.0, -3.0, -4.0, -6.0])


def pack_weight(w, fmt):
    k, n = w.shape
    w = f64(np.asarray(w, np.float32).astype(ml_dtypes.bfloat16)).reshape(k // 32, 32, n)
    amax = np.abs(w).max(1)
    if fmt == "e4m3":
        byte = np.frexp(amax)[1] - 1 + 127 - 7
    else:
        mant, ex = np.frexp(amax / 6.0)
        byte = np.where(mant > 0.5, ex, ex - 1) + 127
    byte = np.clip(np.where(amax > 0, byte, 1), 1, 254)
    scaled = (w * np.exp2(127.0 - byte)[:, None, :]).reshape(k, n).astype(np.float32)
    by_word = np.ascontiguousarray(scaled.reshape(k // 512, 128, 4, n).transpose(0, 1, 3, 2))
    if fmt == "e4m3":
        words = by_word.astype(ml_dtypes.float8_e4m3fn).view(np.uint8)
    else:
        c = by_word.astype(ml_dtypes.float4_e2m1fn).view(np.uint8) & 0xF
        words = (c[..., 0::2] | (c[..., 1::2] << 4)).reshape(k // 512, 128, 2 * n)
    return np.ascontiguousarray(words), np.ascontiguousarray(byte.astype(np.uint8).reshape(k // 512, 16, n))


def unpack_weight(words, scales, fmt):
    g, _, n = scales.shape
    words = np.ascontiguousarray(words).reshape(g, 128, n, -1)
    if fmt == "e4m3":
        vals = words.view(ml_dtypes.float8_e4m3fn).astype(np.float64)
    else:
        nib = np.empty((g, 128, n, 4), np.uint8)
        nib[..., 0::2] = words & 0xF
        nib[..., 1::2] = words >> 4
        vals = E2M1[nib]
    vals = vals * np.repeat(np.exp2(scales.astype(np.float64) - 127.0), 8, axis=1)[..., None]
    return vals.transpose(0, 1, 3, 2).reshape(g * 512, n)


def gelu(v):
    return 0.5 * v * (1.0 + np.tanh(np.sqrt(2.0 / np.pi) * (v + 0.044715 * v**3)))


K, H, N, T, S, P = 512, 1024, 512, 4096, 1024, 512


def setup_inputs():
    n = np.random.standard_normal
    s = mx_kscale(K)[:, None]
    u = mx_kscale(H)[:, None]
    tab_words, tab_scales = pack_weight(n((K, T)) * s, "e4m3")
    w2_words, w2_scales = pack_weight(n((K, H)) / np.sqrt(K) / s, "e4m3")
    w3_words, w3_scales = pack_weight(n((K, H)) / np.sqrt(K) / s, "e2m1")
    wo_words, wo_scales = pack_weight(n((H, N)) / np.sqrt(H) / u, "e2m1")
    return {
        "tab_words": tab_words, "tab_scales": tab_scales,
        "offs": striped(np.random.permutation(T)[:S]),
        "pos1": striped(np.random.permutation(S)[:P]),
        "pos2": striped(np.random.permutation(S)[:P]),
        "w1": (n((K, H)) / np.sqrt(K) / s).astype(np.float32),
        "w2_words": w2_words, "w2_scales": w2_scales,
        "w3_words": w3_words, "w3_scales": w3_scales,
        "gain": (np.exp(0.3 * n(H)) * u[:, 0]).astype(np.float32),
        "base": (0.8 * n(H) * u[:, 0]).astype(np.float32),
        "organ": np.exp(0.4 * n(H)).astype(np.float32),
        "wt": (n((H, N)) / np.sqrt(H) / u).astype(np.float32),
        "wo_words": wo_words, "wo_scales": wo_scales,
        "emph": np.exp(0.4 * n((N, P))).astype(np.float32),
    }


def reference(tab_words, tab_scales, offs, pos1, pos2, w1, w2_words, w2_scales, w3_words, w3_scales,
              gain, base, organ, wt, wo_words, wo_scales, emph):
    v = unpack_weight(tab_words, tab_scales, "e4m3")[:, unstriped(offs)]
    e1 = mxq(f64(w1), 0, "e4m3").T @ v
    e2 = unpack_weight(w2_words, w2_scales, "e4m3").T @ v
    e3 = unpack_weight(w3_words, w3_scales, "e2m1").T @ v
    h = np.minimum(np.maximum(e1, e2), e3) * f64(gain)[:, None]
    xa = h[:, unstriped(pos1)] + f64(base)[:, None]
    xb = h[:, unstriped(pos2)] * f64(organ)[:, None]
    y = (mxq(f64(wt), 0, "e4m3").T @ mxq(xa, 0, "e4m3")
              + unpack_weight(wo_words, wo_scales, "e2m1").T @ mxq(xb, 0, "e4m3"))
    return y * f64(emph)

@@ -1,0 +1,281 @@
+from contextlib import ExitStack
+
+import concourse.mybir as mybir
+
+K, H, N, T, S, PAIRS = 512, 1024, 512, 4096, 1024, 512
+FLOPS = 2 * (3 * K * H * S + 2 * H * N * PAIRS)
+
+F32 = mybir.dt.float32
+BF16 = mybir.dt.bfloat16
+I32 = mybir.dt.int32
+U32 = mybir.dt.uint32
+U16 = mybir.dt.uint16
+U8 = mybir.dt.uint8
+FP8X4 = mybir.dt.float8_e4m3fn_x4
+FP4X4 = mybir.dt.float4_e2m1fn_x4
+ALU = mybir.AluOpType
+ACT = mybir.ActivationFunctionType
+
+P = 128
+PACK = 4
+PASS = P * PACK
+BANK = 512
+BLOCKS = H // PASS
+HALF = PAIRS // 2
+W2_PLANE = 4
+VECTOR_SHARE = 80
+WT_PIECE = 256
+
+
+def tile_list_plan_segment_scores_kernel(
+    tc, tab_words, tab_scales, offs, pos1, pos2, w1, w2_words, w2_scales, w3_words, w3_scales,
+    gain, base, organ, wt, wo_words, wo_scales, emph, out,
+):
+    nc = tc.nc
+    with ExitStack() as ctx:
+        held = ctx.enter_context(tc.tile_pool(name="held", bufs=1))
+        ring = ctx.enter_context(tc.tile_pool(name="ring", bufs=4))
+        psum = ctx.enter_context(tc.psum_pool(name="psum", bufs=1))
+
+        def load_scale_rows(queue, plane, first_row, rows):
+            for r in range(4):
+                queue.dma_start(out=plane[first_row + r : P : 32], in_=rows(r))
+
+        tab_plane = held.tile([P, T], U8, name="tab_plane", align_bytes=64)
+        nc.vector.memset(tab_plane[:].bitcast(I32), 0)
+        w_planes_raw = held.tile([P, H], U8, name="w_planes_raw", tag="planes_raw", align_bytes=64)
+        nc.gpsimd.memset(w_planes_raw[:].bitcast(I32), 0)
+
+        idx = held.tile([P, S // 16], U16, name="idx")
+        p1 = held.tile([P, PAIRS // 16], U16, name="p1")
+        p2 = held.tile([P, PAIRS // 16], U16, name="p2")
+        nc.sync.dma_start(idx[:], offs)
+        nc.sync.dma_start(p1[:], pos1)
+        nc.sync.dma_start(p2[:], pos2)
+        load_scale_rows(nc.scalar, tab_plane[:].bitcast(I32), 0, lambda r: tab_scales[0, r:16:4, :].bitcast(I32))
+        tab = held.tile([P, T], U32, name="tab", tag="tab", align_bytes=64)
+        nc.sync.dma_start(out=tab[:].bitcast(I32), in_=tab_words[0].rearrange("p t i -> p (t i)").bitcast(I32))
+        load_scale_rows(nc.gpsimd, w_planes_raw[:].bitcast(I32), W2_PLANE, lambda r: w2_scales[0, r:16:4, :].bitcast(I32))
+        load_scale_rows(nc.gpsimd, w_planes_raw[:].bitcast(I32), 0, lambda r: w3_scales[0, r:16:4, :].bitcast(I32))
+
+        w2_codes = held.tile([P, H], U32, name="w2_codes", align_bytes=64)
+        w3_codes = held.tile([P, H], U16, name="w3_codes", align_bytes=64)
+        w1_codes = held.tile([P, H], U32, name="w1_codes", align_bytes=64)
+        w1_plane = held.tile([P, H], U8, name="w1_plane", align_bytes=64)
+        w2_rows = w2_words[0].rearrange("p c i -> p (c i)").bitcast(I32)
+
+        def deal(engine_copy, dst, src):
+            engine_copy(out=dst.rearrange("p (t m) -> p m t", t=PACK), in_=src.rearrange("p (m t) -> p m t", t=PACK))
+
+        def load_w2(b):
+            raw = held.tile([P, PASS], U32, name="w2_raw", tag="words_raw", align_bytes=64)
+            nc.sync.dma_start(out=raw[:].bitcast(I32), in_=w2_rows[:, b * PASS : (b + 1) * PASS])
+            return raw
+
+        def load_rows(rows):
+            raw = held.tile([P, PACK, PASS], F32, name="rows_raw", tag="rows_raw", align_bytes=64)
+            nc.sync.dma_start(out=raw[:], in_=rows.rearrange("(p j) c -> p j c", j=PACK))
+            return raw
+
+        w2_raw = load_w2(0)
+        w3_raw = held.tile([P, H], U16, name="w3_raw", tag="w3_raw", align_bytes=64)
+        nc.sync.dma_start(out=w3_raw[:].bitcast(I32), in_=w3_words[0].bitcast(I32))
+        w1_raw = load_rows(w1[:, 0:PASS])
+
+        v_plane = held.tile([P, S], U8, name="v_plane", align_bytes=64)
+        v_codes = held.tile([P, S], U32, name="v_codes", align_bytes=64)
+        nc.vector.tensor_copy(v_plane[:], tab_plane[:].indirect(idx[:]))
+        for s in range(S // BANK):
+            nc.vector.tensor_copy(
+                v_codes[:, s * BANK : (s + 1) * BANK], tab[:].indirect(idx[:, s * BANK // 16 : (s + 1) * BANK // 16])
+            )
+
+        deal(nc.scalar.copy, w2_codes[:, 0:PASS], w2_raw[:])
+        for b in range(BLOCKS):
+            deal(nc.scalar.copy, w3_codes[:, b * PASS : (b + 1) * PASS], w3_raw[:, b * PASS : (b + 1) * PASS])
+        w_planes = held.tile([P, H], U8, name="w_planes", tag="tab", align_bytes=64)
+        nc.vector.tensor_copy(
+            out=w_planes[:].rearrange("p (b t m) -> p b m t", b=BLOCKS, t=PACK),
+            in_=w_planes_raw[:].rearrange("p (b m t) -> p b m t", b=BLOCKS, t=PACK),
+        )
+
+        def round_w1(raw, vector_share):
+            grouped = held.tile([P, PASS * PACK], BF16, name="w1_grouped", tag="w_grouped", align_bytes=64)
+            dst = grouped[:].rearrange("p (t m j) -> p m t j", t=PACK, j=PACK)
+            src = raw[:].rearrange("p j (m t) -> p m t j", t=PACK)
+            if vector_share:
+                nc.vector.tensor_copy(out=dst[:, 0:vector_share], in_=src[:, 0:vector_share])
+                nc.scalar.copy(out=dst[:, vector_share:P], in_=src[:, vector_share:P])
+            else:
+                for m0 in range(0, P, P // 2):
+                    nc.scalar.copy(out=dst[:, m0 : m0 + P // 2], in_=src[:, m0 : m0 + P // 2])
+            return grouped
+
+        def quantize(codes, plane, grouped):
+            nc.vector.quantize_mx(out=codes.bitcast(FP8X4), scales=plane, in_=grouped)
+
+        grouped = round_w1(w1_raw, VECTOR_SHARE)
+        quantize(w1_codes[:, 0:P], w1_plane[:, 0:P], grouped[:, 0 : P * PACK])
+        quantize(w1_codes[:, P:PASS], w1_plane[:, P:PASS], grouped[:, P * PACK : PASS * PACK])
+
+        vecs = held.tile([P, 3, BLOCKS * PACK], F32, name="vecs", tag="w3_raw", align_bytes=64)
+        for row, vec in enumerate((gain, base, organ)):
+            nc.sync.dma_start(
+                out=vecs[:, row, :].rearrange("p (b t) -> p b t", t=PACK), in_=vec.rearrange("(b p t) -> p b t", p=P, t=PACK)
+            )
+        gain_organ = held.tile([P, BLOCKS * PACK], F32, name="gain_organ")
+        nc.gpsimd.tensor_tensor(gain_organ[:], vecs[:, 0, :], vecs[:, 2, :], ALU.mult)
+        w2_raw = load_w2(1)
+        w1_raw = load_rows(w1[:, PASS:H])
+
+        wt_codes = held.tile([P, BLOCKS, N], U32, name="wt_codes", align_bytes=64)
+        wt_plane = held.tile([P, BLOCKS, N], U8, name="wt_plane", align_bytes=64)
+
+        def prepare_second_block():
+            deal(nc.scalar.copy, w2_codes[:, PASS:H], w2_raw[:])
+            second = round_w1(w1_raw, 0)
+            quantize(w1_codes[:, PASS:H], w1_plane[:, PASS:H], second[:])
+
+        def prepare_wt(b):
+            raw = load_rows(wt[b * PASS : (b + 1) * PASS, :])
+            wt_grouped = held.tile([P, N, PACK], BF16, name="wt_grouped", tag="w_grouped", align_bytes=64)
+            for n0 in range(0, N, WT_PIECE):
+                nc.scalar.copy(
+                    out=wt_grouped[:, n0 : n0 + WT_PIECE, :], in_=raw[:, :, n0 : n0 + WT_PIECE].rearrange("p j n -> p n j")
+                )
+            quantize(wt_codes[:, b, :], wt_plane[:, b, :], wt_grouped[:].rearrange("p n j -> p (n j)"))
+
+        q_tiles = [held.tile([P, S], F32, name=f"q{i}", align_bytes=64) for i in range(BLOCKS * PACK)]
+        xa_rows = [held.tile([P, PACK, PAIRS], BF16, name=f"xa_rows{b}", align_bytes=64) for b in range(BLOCKS)]
+        xb_rows = [held.tile([P, PACK, PAIRS], BF16, name=f"xb_rows{b}", align_bytes=64) for b in range(BLOCKS)]
+        xa_codes = held.tile([P, BLOCKS, PAIRS], U32, name="xa_codes", align_bytes=64)
+        xb_codes = held.tile([P, BLOCKS, PAIRS], U32, name="xb_codes", align_bytes=64)
+        xa_plane = held.tile([P, BLOCKS, PAIRS], U8, name="xa_plane", align_bytes=64)
+        xb_plane = held.tile([P, BLOCKS, PAIRS], U8, name="xb_plane", align_bytes=64)
+
+        def first_stage(i):
+            cols = slice(i * P, (i + 1) * P)
+            larger = []
+            limits = []
+            for s in range(S // BANK):
+                seg = slice(s * BANK, (s + 1) * BANK)
+                moving = dict(rhs=v_codes[:, seg].bitcast(FP8X4), rhs_scale=v_plane[:, seg], start=True, stop=True)
+                e2 = psum.tile([P, BANK], F32, name="e2", tag="e2", bufs=2)
+                nc.tensor.matmul_mx(out=e2[:], lhsT=w2_codes[:, cols].bitcast(FP8X4), lhsT_scale=w_planes[W2_PLANE:P, cols], **moving)
+                e1 = psum.tile([P, BANK], F32, name="e1", tag="e1", bufs=3)
+                nc.tensor.matmul_mx(out=e1[:], lhsT=w1_codes[:, cols].bitcast(FP8X4), lhsT_scale=w1_plane[:, cols], **moving)
+                e3 = psum.tile([P, BANK], F32, name="e3", tag="e3", bufs=3)
+                nc.tensor.matmul_mx(out=e3[:], lhsT=w3_codes[:, cols].bitcast(FP4X4), lhsT_scale=w_planes[:, cols], **moving)
+                e2_sb = ring.tile([P, BANK], F32, name="e2_sb", align_bytes=64)
+                nc.scalar.copy(out=e2_sb[:], in_=e2[:])
+                big = ring.tile([P, BANK], F32, name="big", align_bytes=64)
+                nc.vector.tensor_tensor(big[:], e1[:], e2_sb[:], ALU.max)
+                larger.append(big)
+                limits.append(e3)
+            for s in range(S // BANK):
+                nc.vector.tensor_tensor(q_tiles[i][:, s * BANK : (s + 1) * BANK], limits[s][:], larger[s][:], ALU.min)
+
+        def pick(i, positions, m0, m1):
+            picked = ring.tile([P, m1 - m0], F32, name="picked", align_bytes=64)
+            nc.vector.tensor_copy(picked[:], q_tiles[i][:].indirect(positions[:, m0 // 16 : m1 // 16]))
+            return picked
+
+        def pick_a(i, on_scalar):
+            picked = pick(i, p1, 0, PAIRS)
+            dst = xa_rows[i // PACK][:, i % PACK, :]
+            if on_scalar:
+                nc.scalar.activation(dst, picked[:], ACT.Identity, bias=vecs[:, 1, i : i + 1], scale=vecs[:, 0, i : i + 1])
+            else:
+                nc.gpsimd.tensor_scalar(dst, picked[:], vecs[:, 0, i : i + 1], vecs[:, 1, i : i + 1], ALU.mult, ALU.add)
+
+        def pick_b(i, m0, m1, on_scalar):
+            picked = pick(i, p2, m0, m1)
+            dst = xb_rows[i // PACK][:, i % PACK, m0:m1]
+            if on_scalar:
+                nc.scalar.activation(dst, picked[:], ACT.Copy, scale=gain_organ[:, i : i + 1])
+            else:
+                nc.gpsimd.tensor_scalar(dst, picked[:], gain_organ[:, i : i + 1], 0.0, ALU.mult, ALU.add)
+
+        def weave_and_quantize(copy, rows, codes, plane, b, m0, m1):
+            woven = ring.tile([P, m1 - m0, PACK], BF16, name="woven", bufs=3, align_bytes=64)
+            copy(
+                out=woven[:].rearrange("p (c i) t -> p c t i", i=4),
+                in_=rows[b][:, :, m0:m1].rearrange("p t (c i) -> p c t i", i=4),
+            )
+            quantize(codes[:, b, m0:m1], plane[:, b, m0:m1], woven[:].rearrange("p m t -> p (m t)"))
+
+        for i in range(BLOCKS * PACK):
+            first_stage(i)
+            if i >= 1:
+                pick_a(i - 1, False)
+                if i - 1 < PACK:
+                    pick_b(i - 1, 0, PAIRS, False)
+            if i == 1:
+                prepare_second_block()
+                wo_codes = held.tile([P, BLOCKS, N], U16, name="wo_codes", tag="words_raw", align_bytes=64)
+                nc.sync.dma_start(out=wo_codes[:].bitcast(I32), in_=wo_words.rearrange("a p c -> p a c").bitcast(I32))
+                wo_plane = held.tile([P, BLOCKS, N], U8, name="wo_plane", tag="planes_raw", align_bytes=64)
+                nc.gpsimd.memset(wo_plane[:].rearrange("p a n -> p (a n)").bitcast(I32), 0)
+                load_scale_rows(
+                    nc.sync, wo_plane[:].bitcast(I32), 0,
+                    lambda r: wo_scales[:, r:16:4, :].rearrange("a q n -> q a n").bitcast(I32),
+                )
+            if i in (2, 3):
+                prepare_wt(i - 2)
+            if i in (PACK, PACK + 1):
+                rows, codes, plane = ((xa_rows, xa_codes, xa_plane), (xb_rows, xb_codes, xb_plane))[i - PACK]
+                for m0 in range(0, PAIRS, HALF):
+                    weave_and_quantize(nc.scalar.copy, rows, codes, plane, 0, m0, m0 + HALF)
+        emph_sb = held.tile([P, N // P, PAIRS], F32, name="emph_sb", tag="rows_raw", align_bytes=64)
+        nc.sync.dma_start(out=emph_sb[:], in_=emph.rearrange("(u p) m -> p u m", p=P))
+
+        last = BLOCKS - 1
+        bank_tags = (("e2", 2), ("e2", 2), ("e1", 3), ("e1", 3), ("e1", 3), ("e3", 3), ("e3", 3), ("e3", 3))
+        sums = {}
+        for half in range(2):
+            for u in range(N // P):
+                tag, bufs = bank_tags[half * (N // P) + u]
+                sums[half, u] = psum.tile([P, HALF], F32, name="sum", tag=tag, bufs=bufs)
+
+        def second_stage(half, b, use_xa):
+            pairs = slice(half * HALF, (half + 1) * HALF)
+            for u in range(N // P):
+                cols = slice(u * P, (u + 1) * P)
+                if use_xa:
+                    nc.tensor.matmul_mx(
+                        out=sums[half, u][:], lhsT=wt_codes[:, b, cols].bitcast(FP8X4), lhsT_scale=wt_plane[:, b, cols],
+                        rhs=xa_codes[:, b, pairs].bitcast(FP8X4), rhs_scale=xa_plane[:, b, pairs], start=(b == 0), stop=False,
+                    )
+                else:
+                    nc.tensor.matmul_mx(
+                        out=sums[half, u][:], lhsT=wo_codes[:, b, cols].bitcast(FP4X4), lhsT_scale=wo_plane[:, b, cols],
+                        rhs=xb_codes[:, b, pairs].bitcast(FP8X4), rhs_scale=xb_plane[:, b, pairs], start=False, stop=(b == last),
+                    )
+
+        def finish(half):
+            pairs = slice(half * HALF, (half + 1) * HALF)
+            scores = held.tile([P, N // P, HALF], F32, name=f"scores{half}", align_bytes=64)
+            for u in range(N // P):
+                nc.vector.tensor_tensor(scores[:, u, :], sums[half, u][:], emph_sb[:, u, pairs], ALU.mult)
+                if u % 2 == 1:
+                    nc.sync.dma_start(
+                        out=out[(u - 1) * P : (u + 1) * P, pairs].rearrange("(u p) m -> p u m", p=P), in_=scores[:, u - 1 : u + 1, :]
+                    )
+
+        for half in range(2):
+            second_stage(half, 0, True)
+            second_stage(half, 0, False)
+        pick_a(BLOCKS * PACK - 1, True)
+        for t in range(PACK):
+            pick_b(last * PACK + t, 0, HALF, True)
+        for half in range(2):
+            weave_and_quantize(nc.scalar.copy, xa_rows, xa_codes, xa_plane, last, half * HALF, (half + 1) * HALF)
+            second_stage(half, last, True)
+        for t in range(PACK):
+            pick_b(last * PACK + t, HALF, PAIRS, True)
+        weave_and_quantize(nc.scalar.copy, xb_rows, xb_codes, xb_plane, last, 0, HALF)
+        second_stage(0, last, False)
+        weave_and_quantize(nc.vector.tensor_copy, xb_rows, xb_codes, xb_plane, last, HALF, PAIRS)
+        second_stage(1, last, False)
+        finish(0)
+        finish(1)

@@ -23,7 +23,6 @@ BANK = 512
 BLOCKS = H // PASS
 HALF = PAIRS // 2
 W2_PLANE = 4
-VECTOR_SHARE = 80
 WT_PIECE = 256
 
 
@@ -37,11 +36,11 @@ def tile_list_plan_segment_scores_kernel(
         ring = ctx.enter_context(tc.tile_pool(name="ring", bufs=4))
         psum = ctx.enter_context(tc.psum_pool(name="psum", bufs=1))
 
-        def load_scale_rows(queue, plane, first_row, rows):
-            for r in range(4):
+        def load_scale_rows(queue, plane, first_row, rows, which=range(4)):
+            for r in which:
                 queue.dma_start(out=plane[first_row + r : P : 32], in_=rows(r))
 
-        tab_plane = held.tile([P, T], U8, name="tab_plane", align_bytes=64)
+        tab_plane = held.tile([P, T], U8, name="tab_plane", tag="tab_plane", align_bytes=64)
         nc.vector.memset(tab_plane[:].bitcast(I32), 0)
         w_planes_raw = held.tile([P, H], U8, name="w_planes_raw", tag="planes_raw", align_bytes=64)
         nc.gpsimd.memset(w_planes_raw[:].bitcast(I32), 0)
@@ -49,23 +48,14 @@ def tile_list_plan_segment_scores_kernel(
         idx = held.tile([P, S // 16], U16, name="idx")
         p1 = held.tile([P, PAIRS // 16], U16, name="p1")
         p2 = held.tile([P, PAIRS // 16], U16, name="p2")
-        nc.sync.dma_start(idx[:], offs)
-        nc.sync.dma_start(p1[:], pos1)
-        nc.sync.dma_start(p2[:], pos2)
-        load_scale_rows(nc.scalar, tab_plane[:].bitcast(I32), 0, lambda r: tab_scales[0, r:16:4, :].bitcast(I32))
-        tab = held.tile([P, T], U32, name="tab", tag="tab", align_bytes=64)
-        nc.sync.dma_start(out=tab[:].bitcast(I32), in_=tab_words[0].rearrange("p t i -> p (t i)").bitcast(I32))
-        load_scale_rows(nc.gpsimd, w_planes_raw[:].bitcast(I32), W2_PLANE, lambda r: w2_scales[0, r:16:4, :].bitcast(I32))
-        load_scale_rows(nc.gpsimd, w_planes_raw[:].bitcast(I32), 0, lambda r: w3_scales[0, r:16:4, :].bitcast(I32))
-
         w2_codes = held.tile([P, H], U32, name="w2_codes", align_bytes=64)
         w3_codes = held.tile([P, H], U16, name="w3_codes", align_bytes=64)
         w1_codes = held.tile([P, H], U32, name="w1_codes", align_bytes=64)
         w1_plane = held.tile([P, H], U8, name="w1_plane", align_bytes=64)
         w2_rows = w2_words[0].rearrange("p c i -> p (c i)").bitcast(I32)
 
-        def deal(engine_copy, dst, src):
-            engine_copy(out=dst.rearrange("p (t m) -> p m t", t=PACK), in_=src.rearrange("p (m t) -> p m t", t=PACK))
+        def deal(dst, src):
+            nc.scalar.copy(out=dst.rearrange("p (t m) -> p m t", t=PACK), in_=src.rearrange("p (m t) -> p m t", t=PACK))
 
         def load_w2(b):
             raw = held.tile([P, PASS], U32, name="w2_raw", tag="words_raw", align_bytes=64)
@@ -77,46 +67,47 @@ def tile_list_plan_segment_scores_kernel(
             nc.sync.dma_start(out=raw[:], in_=rows.rearrange("(p j) c -> p j c", j=PACK))
             return raw
 
+        nc.sync.dma_start(idx[:], offs)
+        load_scale_rows(nc.sync, tab_plane[:].bitcast(I32), 0, lambda r: tab_scales[0, r:16:4, :].bitcast(I32))
+        load_scale_rows(nc.sync, w_planes_raw[:].bitcast(I32), W2_PLANE, lambda r: w2_scales[0, r:16:4, :].bitcast(I32), range(2))
+        w1_raw = load_rows(w1[:, 0:PASS])
+        load_scale_rows(nc.sync, w_planes_raw[:].bitcast(I32), W2_PLANE, lambda r: w2_scales[0, r:16:4, :].bitcast(I32), range(2, 4))
+        load_scale_rows(nc.sync, w_planes_raw[:].bitcast(I32), 0, lambda r: w3_scales[0, r:16:4, :].bitcast(I32))
+        tab = held.tile([P, T], U32, name="tab", align_bytes=64)
+        nc.sync.dma_start(out=tab[:].bitcast(I32), in_=tab_words[0].rearrange("p t i -> p (t i)").bitcast(I32))
         w2_raw = load_w2(0)
         w3_raw = held.tile([P, H], U16, name="w3_raw", tag="w3_raw", align_bytes=64)
         nc.sync.dma_start(out=w3_raw[:].bitcast(I32), in_=w3_words[0].bitcast(I32))
-        w1_raw = load_rows(w1[:, 0:PASS])
+        nc.sync.dma_start(p1[:], pos1)
+        nc.sync.dma_start(p2[:], pos2)
 
-        v_plane = held.tile([P, S], U8, name="v_plane", align_bytes=64)
-        v_codes = held.tile([P, S], U32, name="v_codes", align_bytes=64)
-        nc.vector.tensor_copy(v_plane[:], tab_plane[:].indirect(idx[:]))
-        for s in range(S // BANK):
-            nc.vector.tensor_copy(
-                v_codes[:, s * BANK : (s + 1) * BANK], tab[:].indirect(idx[:, s * BANK // 16 : (s + 1) * BANK // 16])
-            )
-
-        deal(nc.scalar.copy, w2_codes[:, 0:PASS], w2_raw[:])
-        for b in range(BLOCKS):
-            deal(nc.scalar.copy, w3_codes[:, b * PASS : (b + 1) * PASS], w3_raw[:, b * PASS : (b + 1) * PASS])
-        w_planes = held.tile([P, H], U8, name="w_planes", tag="tab", align_bytes=64)
-        nc.vector.tensor_copy(
-            out=w_planes[:].rearrange("p (b t m) -> p b m t", b=BLOCKS, t=PACK),
-            in_=w_planes_raw[:].rearrange("p (b m t) -> p b m t", b=BLOCKS, t=PACK),
-        )
-
-        def round_w1(raw, vector_share):
+        def round_w1(raw):
             grouped = held.tile([P, PASS * PACK], BF16, name="w1_grouped", tag="w_grouped", align_bytes=64)
             dst = grouped[:].rearrange("p (t m j) -> p m t j", t=PACK, j=PACK)
             src = raw[:].rearrange("p j (m t) -> p m t j", t=PACK)
-            if vector_share:
-                nc.vector.tensor_copy(out=dst[:, 0:vector_share], in_=src[:, 0:vector_share])
-                nc.scalar.copy(out=dst[:, vector_share:P], in_=src[:, vector_share:P])
-            else:
-                for m0 in range(0, P, P // 2):
-                    nc.scalar.copy(out=dst[:, m0 : m0 + P // 2], in_=src[:, m0 : m0 + P // 2])
+            for m0 in range(0, P, P // 2):
+                nc.scalar.copy(out=dst[:, m0 : m0 + P // 2], in_=src[:, m0 : m0 + P // 2])
             return grouped
 
         def quantize(codes, plane, grouped):
             nc.vector.quantize_mx(out=codes.bitcast(FP8X4), scales=plane, in_=grouped)
 
-        grouped = round_w1(w1_raw, VECTOR_SHARE)
-        quantize(w1_codes[:, 0:P], w1_plane[:, 0:P], grouped[:, 0 : P * PACK])
-        quantize(w1_codes[:, P:PASS], w1_plane[:, P:PASS], grouped[:, P * PACK : PASS * PACK])
+        v_plane = held.tile([P, S], U8, name="v_plane", align_bytes=64)
+        v_codes = held.tile([P, S], U32, name="v_codes", align_bytes=64)
+        nc.vector.tensor_copy(v_plane[:], tab_plane[:].indirect(idx[:]))
+        w_planes = held.tile([P, H], U8, name="w_planes", tag="tab_plane", align_bytes=64)
+        nc.vector.tensor_copy(
+            out=w_planes[:].rearrange("p (b t m) -> p b m t", b=BLOCKS, t=PACK),
+            in_=w_planes_raw[:].rearrange("p (b m t) -> p b m t", b=BLOCKS, t=PACK),
+        )
+        quantize(w1_codes[:, 0:PASS], w1_plane[:, 0:PASS], round_w1(w1_raw)[:])
+        for s in range(S // BANK):
+            nc.vector.tensor_copy(
+                v_codes[:, s * BANK : (s + 1) * BANK], tab[:].indirect(idx[:, s * BANK // 16 : (s + 1) * BANK // 16])
+            )
+        deal(w2_codes[:, 0:PASS], w2_raw[:])
+        for b in range(BLOCKS):
+            deal(w3_codes[:, b * PASS : (b + 1) * PASS], w3_raw[:, b * PASS : (b + 1) * PASS])
 
         vecs = held.tile([P, 3, BLOCKS * PACK], F32, name="vecs", tag="w3_raw", align_bytes=64)
         for row, vec in enumerate((gain, base, organ)):
@@ -132,8 +123,8 @@ def tile_list_plan_segment_scores_kernel(
         wt_plane = held.tile([P, BLOCKS, N], U8, name="wt_plane", align_bytes=64)
 
         def prepare_second_block():
-            deal(nc.scalar.copy, w2_codes[:, PASS:H], w2_raw[:])
-            second = round_w1(w1_raw, 0)
+            deal(w2_codes[:, PASS:H], w2_raw[:])
+            second = round_w1(w1_raw)
             quantize(w1_codes[:, PASS:H], w1_plane[:, PASS:H], second[:])
 
         def prepare_wt(b):
@@ -146,8 +137,8 @@ def tile_list_plan_segment_scores_kernel(
             quantize(wt_codes[:, b, :], wt_plane[:, b, :], wt_grouped[:].rearrange("p n j -> p (n j)"))
 
         q_tiles = [held.tile([P, S], F32, name=f"q{i}", align_bytes=64) for i in range(BLOCKS * PACK)]
-        xa_rows = [held.tile([P, PACK, PAIRS], BF16, name=f"xa_rows{b}", align_bytes=64) for b in range(BLOCKS)]
-        xb_rows = [held.tile([P, PACK, PAIRS], BF16, name=f"xb_rows{b}", align_bytes=64) for b in range(BLOCKS)]
+        xa_rows = [held.tile([P, 2, PAIRS, 2], BF16, name=f"xa_rows{b}", align_bytes=64) for b in range(BLOCKS)]
+        xb_rows = [held.tile([P, 2, PAIRS, 2], BF16, name=f"xb_rows{b}", align_bytes=64) for b in range(BLOCKS)]
         xa_codes = held.tile([P, BLOCKS, PAIRS], U32, name="xa_codes", align_bytes=64)
         xb_codes = held.tile([P, BLOCKS, PAIRS], U32, name="xb_codes", align_bytes=64)
         xa_plane = held.tile([P, BLOCKS, PAIRS], U8, name="xa_plane", align_bytes=64)
@@ -182,7 +173,7 @@ def tile_list_plan_segment_scores_kernel(
 
         def pick_a(i, on_scalar):
             picked = pick(i, p1, 0, PAIRS)
-            dst = xa_rows[i // PACK][:, i % PACK, :]
+            dst = xa_rows[i // PACK][:, i % PACK // 2, :, i % 2]
             if on_scalar:
                 nc.scalar.activation(dst, picked[:], ACT.Identity, bias=vecs[:, 1, i : i + 1], scale=vecs[:, 0, i : i + 1])
             else:
@@ -190,24 +181,22 @@ def tile_list_plan_segment_scores_kernel(
 
         def pick_b(i, m0, m1, on_scalar):
             picked = pick(i, p2, m0, m1)
-            dst = xb_rows[i // PACK][:, i % PACK, m0:m1]
+            dst = xb_rows[i // PACK][:, i % PACK // 2, m0:m1, i % 2]
             if on_scalar:
                 nc.scalar.activation(dst, picked[:], ACT.Copy, scale=gain_organ[:, i : i + 1])
             else:
                 nc.gpsimd.tensor_scalar(dst, picked[:], gain_organ[:, i : i + 1], 0.0, ALU.mult, ALU.add)
 
         def weave_and_quantize(copy, rows, codes, plane, b, m0, m1):
-            woven = ring.tile([P, m1 - m0, PACK], BF16, name="woven", bufs=3, align_bytes=64)
-            copy(
-                out=woven[:].rearrange("p (c i) t -> p c t i", i=4),
-                in_=rows[b][:, :, m0:m1].rearrange("p t (c i) -> p c t i", i=4),
-            )
-            quantize(codes[:, b, m0:m1], plane[:, b, m0:m1], woven[:].rearrange("p m t -> p (m t)"))
+            woven = ring.tile([P, (m1 - m0) * PACK], BF16, name="woven", bufs=3, align_bytes=64)
+            words = rows[b][:].rearrange("p u m e -> p u (m e)").bitcast(U32)
+            copy(out=woven[:].bitcast(U32).rearrange("p (m u) -> p m u", u=2), in_=words[:, :, m0:m1].rearrange("p u m -> p m u"))
+            quantize(codes[:, b, m0:m1], plane[:, b, m0:m1], woven[:])
 
         for i in range(BLOCKS * PACK):
             first_stage(i)
             if i >= 1:
-                pick_a(i - 1, False)
+                pick_a(i - 1, i == BLOCKS * PACK - 1)
                 if i - 1 < PACK:
                     pick_b(i - 1, 0, PAIRS, False)
             if i == 1:
@@ -224,58 +213,66 @@ def tile_list_plan_segment_scores_kernel(
                 prepare_wt(i - 2)
             if i in (PACK, PACK + 1):
                 rows, codes, plane = ((xa_rows, xa_codes, xa_plane), (xb_rows, xb_codes, xb_plane))[i - PACK]
-                for m0 in range(0, PAIRS, HALF):
-                    weave_and_quantize(nc.scalar.copy, rows, codes, plane, 0, m0, m0 + HALF)
+                weave_and_quantize(nc.scalar.copy, rows, codes, plane, 0, 0, PAIRS)
         emph_sb = held.tile([P, N // P, PAIRS], F32, name="emph_sb", tag="rows_raw", align_bytes=64)
         nc.sync.dma_start(out=emph_sb[:], in_=emph.rearrange("(u p) m -> p u m", p=P))
 
         last = BLOCKS - 1
-        bank_tags = (("e2", 2), ("e2", 2), ("e1", 3), ("e1", 3), ("e1", 3), ("e3", 3), ("e3", 3), ("e3", 3))
+        tiles_n = N // P
+        chunks = ((0, 256), (256, 384), (384, 512))
         sums = {}
-        for half in range(2):
-            for u in range(N // P):
-                tag, bufs = bank_tags[half * (N // P) + u]
-                sums[half, u] = psum.tile([P, HALF], F32, name="sum", tag=tag, bufs=bufs)
+        opens = {}
+        closes = {}
+        spare_tags = [("e2", 2), ("e2", 2), ("e1", 3), ("e3", 3)]
+        for c, (m0, m1) in enumerate(chunks):
+            per_bank = BANK // (m1 - m0)
+            for u0 in range(0, tiles_n, per_bank):
+                tag, bufs = spare_tags.pop(0)
+                bank = psum.tile([P, per_bank, m1 - m0], F32, name="sum", tag=tag, bufs=bufs)
+                for u in range(u0, u0 + per_bank):
+                    sums[c, u] = bank
+                    opens[c, u] = u == u0
+                    closes[c, u] = u == u0 + per_bank - 1
 
-        def second_stage(half, b, use_xa):
-            pairs = slice(half * HALF, (half + 1) * HALF)
-            for u in range(N // P):
+        def second_stage(c, b, use_xa):
+            m0, m1 = chunks[c]
+            per_bank = BANK // (m1 - m0)
+            for u in range(tiles_n):
                 cols = slice(u * P, (u + 1) * P)
                 if use_xa:
                     nc.tensor.matmul_mx(
-                        out=sums[half, u][:], lhsT=wt_codes[:, b, cols].bitcast(FP8X4), lhsT_scale=wt_plane[:, b, cols],
-                        rhs=xa_codes[:, b, pairs].bitcast(FP8X4), rhs_scale=xa_plane[:, b, pairs], start=(b == 0), stop=False,
+                        out=sums[c, u][:, u % per_bank, :], lhsT=wt_codes[:, b, cols].bitcast(FP8X4), lhsT_scale=wt_plane[:, b, cols],
+                        rhs=xa_codes[:, b, m0:m1].bitcast(FP8X4), rhs_scale=xa_plane[:, b, m0:m1],
+                        start=(b == 0 and opens[c, u]), stop=False,
                     )
                 else:
                     nc.tensor.matmul_mx(
-                        out=sums[half, u][:], lhsT=wo_codes[:, b, cols].bitcast(FP4X4), lhsT_scale=wo_plane[:, b, cols],
-                        rhs=xb_codes[:, b, pairs].bitcast(FP8X4), rhs_scale=xb_plane[:, b, pairs], start=False, stop=(b == last),
+                        out=sums[c, u][:, u % per_bank, :], lhsT=wo_codes[:, b, cols].bitcast(FP4X4), lhsT_scale=wo_plane[:, b, cols],
+                        rhs=xb_codes[:, b, m0:m1].bitcast(FP8X4), rhs_scale=xb_plane[:, b, m0:m1],
+                        start=False, stop=(b == last and closes[c, u]),
                     )
 
-        def finish(half):
-            pairs = slice(half * HALF, (half + 1) * HALF)
-            scores = held.tile([P, N // P, HALF], F32, name=f"scores{half}", align_bytes=64)
-            for u in range(N // P):
-                nc.vector.tensor_tensor(scores[:, u, :], sums[half, u][:], emph_sb[:, u, pairs], ALU.mult)
-                if u % 2 == 1:
-                    nc.sync.dma_start(
-                        out=out[(u - 1) * P : (u + 1) * P, pairs].rearrange("(u p) m -> p u m", p=P), in_=scores[:, u - 1 : u + 1, :]
-                    )
+        def finish(c):
+            m0, m1 = chunks[c]
+            per_bank = BANK // (m1 - m0)
+            for u0 in range(0, tiles_n, per_bank):
+                scores = held.tile([P, per_bank, m1 - m0], F32, name=f"scores{c}_{u0}", align_bytes=64)
+                nc.vector.tensor_tensor(scores[:], sums[c, u0][:], emph_sb[:, u0 : u0 + per_bank, m0:m1], ALU.mult)
+                nc.sync.dma_start(
+                    out=out[u0 * P : (u0 + per_bank) * P, m0:m1].rearrange("(u p) m -> p u m", p=P), in_=scores[:]
+                )
 
-        for half in range(2):
-            second_stage(half, 0, True)
-            second_stage(half, 0, False)
+        for c in range(len(chunks)):
+            second_stage(c, 0, True)
+            second_stage(c, 0, False)
         pick_a(BLOCKS * PACK - 1, True)
-        for t in range(PACK):
-            pick_b(last * PACK + t, 0, HALF, True)
-        for half in range(2):
-            weave_and_quantize(nc.scalar.copy, xa_rows, xa_codes, xa_plane, last, half * HALF, (half + 1) * HALF)
-            second_stage(half, last, True)
-        for t in range(PACK):
-            pick_b(last * PACK + t, HALF, PAIRS, True)
-        weave_and_quantize(nc.scalar.copy, xb_rows, xb_codes, xb_plane, last, 0, HALF)
-        second_stage(0, last, False)
-        weave_and_quantize(nc.vector.tensor_copy, xb_rows, xb_codes, xb_plane, last, HALF, PAIRS)
-        second_stage(1, last, False)
-        finish(0)
-        finish(1)
+        weave_and_quantize(nc.scalar.copy, xa_rows, xa_codes, xa_plane, last, 0, PAIRS)
+        for c in range(len(chunks)):
+            second_stage(c, last, True)
+        for c, (m0, m1) in enumerate(chunks):
+            for t in range(PACK):
+                pick_b(last * PACK + t, m0, m1, True)
+            weave_and_quantize(nc.scalar.copy, xb_rows, xb_codes, xb_plane, last, m0, m1)
+            second_stage(c, last, False)
+        for c in range(len(chunks)):
+            finish(c)

from contextlib import ExitStack

import concourse.mybir as mybir

K, H, N, T, S, PAIRS = 512, 1024, 512, 4096, 1024, 512
FLOPS = 2 * (3 * K * H * S + 2 * H * N * PAIRS)

F32 = mybir.dt.float32
BF16 = mybir.dt.bfloat16
I32 = mybir.dt.int32
U32 = mybir.dt.uint32
U16 = mybir.dt.uint16
U8 = mybir.dt.uint8
FP8X4 = mybir.dt.float8_e4m3fn_x4
FP4X4 = mybir.dt.float4_e2m1fn_x4
ALU = mybir.AluOpType
ACT = mybir.ActivationFunctionType

P = 128
PACK = 4
PASS = P * PACK
BANK = 512
BLOCKS = H // PASS
HALF = PAIRS // 2
W2_PLANE = 4
WT_PIECE = 256


def tile_list_plan_segment_scores_kernel(
    tc, tab_words, tab_scales, offs, pos1, pos2, w1, w2_words, w2_scales, w3_words, w3_scales,
    gain, base, organ, wt, wo_words, wo_scales, emph, out,
):
    nc = tc.nc
    with ExitStack() as ctx:
        held = ctx.enter_context(tc.tile_pool(name="held", bufs=1))
        ring = ctx.enter_context(tc.tile_pool(name="ring", bufs=4))
        psum = ctx.enter_context(tc.psum_pool(name="psum", bufs=1))

        def load_scale_rows(queue, plane, first_row, rows, which=range(4)):
            for r in which:
                queue.dma_start(out=plane[first_row + r : P : 32], in_=rows(r))

        tab_plane = held.tile([P, T], U8, name="tab_plane", tag="tab_plane", align_bytes=64)
        nc.vector.memset(tab_plane[:].bitcast(I32), 0)
        w_planes_raw = held.tile([P, H], U8, name="w_planes_raw", tag="planes_raw", align_bytes=64)
        nc.gpsimd.memset(w_planes_raw[:].bitcast(I32), 0)

        idx = held.tile([P, S // 16], U16, name="idx")
        p1 = held.tile([P, PAIRS // 16], U16, name="p1")
        p2 = held.tile([P, PAIRS // 16], U16, name="p2")
        w2_codes = held.tile([P, H], U32, name="w2_codes", align_bytes=64)
        w3_codes = held.tile([P, H], U16, name="w3_codes", align_bytes=64)
        w1_codes = held.tile([P, H], U32, name="w1_codes", align_bytes=64)
        w1_plane = held.tile([P, H], U8, name="w1_plane", align_bytes=64)
        w2_rows = w2_words[0].rearrange("p c i -> p (c i)").bitcast(I32)

        def deal(dst, src):
            nc.scalar.copy(out=dst.rearrange("p (t m) -> p m t", t=PACK), in_=src.rearrange("p (m t) -> p m t", t=PACK))

        def load_w2(b):
            raw = held.tile([P, PASS], U32, name="w2_raw", tag="words_raw", align_bytes=64)
            nc.sync.dma_start(out=raw[:].bitcast(I32), in_=w2_rows[:, b * PASS : (b + 1) * PASS])
            return raw

        def load_rows(rows):
            raw = held.tile([P, PACK, PASS], F32, name="rows_raw", tag="rows_raw", align_bytes=64)
            nc.sync.dma_start(out=raw[:], in_=rows.rearrange("(p j) c -> p j c", j=PACK))
            return raw

        nc.sync.dma_start(idx[:], offs)
        load_scale_rows(nc.sync, tab_plane[:].bitcast(I32), 0, lambda r: tab_scales[0, r:16:4, :].bitcast(I32))
        load_scale_rows(nc.sync, w_planes_raw[:].bitcast(I32), W2_PLANE, lambda r: w2_scales[0, r:16:4, :].bitcast(I32), range(2))
        w1_raw = load_rows(w1[:, 0:PASS])
        load_scale_rows(nc.sync, w_planes_raw[:].bitcast(I32), W2_PLANE, lambda r: w2_scales[0, r:16:4, :].bitcast(I32), range(2, 4))
        load_scale_rows(nc.sync, w_planes_raw[:].bitcast(I32), 0, lambda r: w3_scales[0, r:16:4, :].bitcast(I32))
        tab = held.tile([P, T], U32, name="tab", align_bytes=64)
        nc.sync.dma_start(out=tab[:].bitcast(I32), in_=tab_words[0].rearrange("p t i -> p (t i)").bitcast(I32))
        w2_raw = load_w2(0)
        w3_raw = held.tile([P, H], U16, name="w3_raw", tag="w3_raw", align_bytes=64)
        nc.sync.dma_start(out=w3_raw[:].bitcast(I32), in_=w3_words[0].bitcast(I32))
        nc.sync.dma_start(p1[:], pos1)
        nc.sync.dma_start(p2[:], pos2)

        def round_w1(raw):
            grouped = held.tile([P, PASS * PACK], BF16, name="w1_grouped", tag="w_grouped", align_bytes=64)
            dst = grouped[:].rearrange("p (t m j) -> p m t j", t=PACK, j=PACK)
            src = raw[:].rearrange("p j (m t) -> p m t j", t=PACK)
            for m0 in range(0, P, P // 2):
                nc.scalar.copy(out=dst[:, m0 : m0 + P // 2], in_=src[:, m0 : m0 + P // 2])
            return grouped

        def quantize(codes, plane, grouped):
            nc.vector.quantize_mx(out=codes.bitcast(FP8X4), scales=plane, in_=grouped)

        v_plane = held.tile([P, S], U8, name="v_plane", align_bytes=64)
        v_codes = held.tile([P, S], U32, name="v_codes", align_bytes=64)
        nc.vector.tensor_copy(v_plane[:], tab_plane[:].indirect(idx[:]))
        w_planes = held.tile([P, H], U8, name="w_planes", tag="tab_plane", align_bytes=64)
        nc.vector.tensor_copy(
            out=w_planes[:].rearrange("p (b t m) -> p b m t", b=BLOCKS, t=PACK),
            in_=w_planes_raw[:].rearrange("p (b m t) -> p b m t", b=BLOCKS, t=PACK),
        )
        quantize(w1_codes[:, 0:PASS], w1_plane[:, 0:PASS], round_w1(w1_raw)[:])
        for s in range(S // BANK):
            nc.vector.tensor_copy(
                v_codes[:, s * BANK : (s + 1) * BANK], tab[:].indirect(idx[:, s * BANK // 16 : (s + 1) * BANK // 16])
            )
        deal(w2_codes[:, 0:PASS], w2_raw[:])
        for b in range(BLOCKS):
            deal(w3_codes[:, b * PASS : (b + 1) * PASS], w3_raw[:, b * PASS : (b + 1) * PASS])

        vecs = held.tile([P, 3, BLOCKS * PACK], F32, name="vecs", tag="w3_raw", align_bytes=64)
        for row, vec in enumerate((gain, base, organ)):
            nc.sync.dma_start(
                out=vecs[:, row, :].rearrange("p (b t) -> p b t", t=PACK), in_=vec.rearrange("(b p t) -> p b t", p=P, t=PACK)
            )
        gain_organ = held.tile([P, BLOCKS * PACK], F32, name="gain_organ")
        nc.gpsimd.tensor_tensor(gain_organ[:], vecs[:, 0, :], vecs[:, 2, :], ALU.mult)
        w2_raw = load_w2(1)
        w1_raw = load_rows(w1[:, PASS:H])

        wt_codes = held.tile([P, BLOCKS, N], U32, name="wt_codes", align_bytes=64)
        wt_plane = held.tile([P, BLOCKS, N], U8, name="wt_plane", align_bytes=64)

        def prepare_second_block():
            deal(w2_codes[:, PASS:H], w2_raw[:])
            second = round_w1(w1_raw)
            quantize(w1_codes[:, PASS:H], w1_plane[:, PASS:H], second[:])

        def prepare_wt(b):
            raw = load_rows(wt[b * PASS : (b + 1) * PASS, :])
            wt_grouped = held.tile([P, N, PACK], BF16, name="wt_grouped", tag="w_grouped", align_bytes=64)
            for n0 in range(0, N, WT_PIECE):
                nc.scalar.copy(
                    out=wt_grouped[:, n0 : n0 + WT_PIECE, :], in_=raw[:, :, n0 : n0 + WT_PIECE].rearrange("p j n -> p n j")
                )
            quantize(wt_codes[:, b, :], wt_plane[:, b, :], wt_grouped[:].rearrange("p n j -> p (n j)"))

        q_tiles = [held.tile([P, S], F32, name=f"q{i}", align_bytes=64) for i in range(BLOCKS * PACK)]
        xa_rows = [held.tile([P, 2, PAIRS, 2], BF16, name=f"xa_rows{b}", align_bytes=64) for b in range(BLOCKS)]
        xb_rows = [held.tile([P, 2, PAIRS, 2], BF16, name=f"xb_rows{b}", align_bytes=64) for b in range(BLOCKS)]
        xa_codes = held.tile([P, BLOCKS, PAIRS], U32, name="xa_codes", align_bytes=64)
        xb_codes = held.tile([P, BLOCKS, PAIRS], U32, name="xb_codes", align_bytes=64)
        xa_plane = held.tile([P, BLOCKS, PAIRS], U8, name="xa_plane", align_bytes=64)
        xb_plane = held.tile([P, BLOCKS, PAIRS], U8, name="xb_plane", align_bytes=64)

        def first_stage(i):
            cols = slice(i * P, (i + 1) * P)
            larger = []
            limits = []
            for s in range(S // BANK):
                seg = slice(s * BANK, (s + 1) * BANK)
                moving = dict(rhs=v_codes[:, seg].bitcast(FP8X4), rhs_scale=v_plane[:, seg], start=True, stop=True)
                e2 = psum.tile([P, BANK], F32, name="e2", tag="e2", bufs=2)
                nc.tensor.matmul_mx(out=e2[:], lhsT=w2_codes[:, cols].bitcast(FP8X4), lhsT_scale=w_planes[W2_PLANE:P, cols], **moving)
                e1 = psum.tile([P, BANK], F32, name="e1", tag="e1", bufs=3)
                nc.tensor.matmul_mx(out=e1[:], lhsT=w1_codes[:, cols].bitcast(FP8X4), lhsT_scale=w1_plane[:, cols], **moving)
                e3 = psum.tile([P, BANK], F32, name="e3", tag="e3", bufs=3)
                nc.tensor.matmul_mx(out=e3[:], lhsT=w3_codes[:, cols].bitcast(FP4X4), lhsT_scale=w_planes[:, cols], **moving)
                e2_sb = ring.tile([P, BANK], F32, name="e2_sb", align_bytes=64)
                nc.scalar.copy(out=e2_sb[:], in_=e2[:])
                big = ring.tile([P, BANK], F32, name="big", align_bytes=64)
                nc.vector.tensor_tensor(big[:], e1[:], e2_sb[:], ALU.max)
                larger.append(big)
                limits.append(e3)
            for s in range(S // BANK):
                nc.vector.tensor_tensor(q_tiles[i][:, s * BANK : (s + 1) * BANK], limits[s][:], larger[s][:], ALU.min)

        def pick(i, positions, m0, m1):
            picked = ring.tile([P, m1 - m0], F32, name="picked", align_bytes=64)
            nc.vector.tensor_copy(picked[:], q_tiles[i][:].indirect(positions[:, m0 // 16 : m1 // 16]))
            return picked

        def pick_a(i, on_scalar):
            picked = pick(i, p1, 0, PAIRS)
            dst = xa_rows[i // PACK][:, i % PACK // 2, :, i % 2]
            if on_scalar:
                nc.scalar.activation(dst, picked[:], ACT.Identity, bias=vecs[:, 1, i : i + 1], scale=vecs[:, 0, i : i + 1])
            else:
                nc.gpsimd.tensor_scalar(dst, picked[:], vecs[:, 0, i : i + 1], vecs[:, 1, i : i + 1], ALU.mult, ALU.add)

        def pick_b(i, m0, m1, on_scalar):
            picked = pick(i, p2, m0, m1)
            dst = xb_rows[i // PACK][:, i % PACK // 2, m0:m1, i % 2]
            if on_scalar:
                nc.scalar.activation(dst, picked[:], ACT.Copy, scale=gain_organ[:, i : i + 1])
            else:
                nc.gpsimd.tensor_scalar(dst, picked[:], gain_organ[:, i : i + 1], 0.0, ALU.mult, ALU.add)

        def weave_and_quantize(copy, rows, codes, plane, b, m0, m1):
            woven = ring.tile([P, (m1 - m0) * PACK], BF16, name="woven", bufs=3, align_bytes=64)
            words = rows[b][:].rearrange("p u m e -> p u (m e)").bitcast(U32)
            copy(out=woven[:].bitcast(U32).rearrange("p (m u) -> p m u", u=2), in_=words[:, :, m0:m1].rearrange("p u m -> p m u"))
            quantize(codes[:, b, m0:m1], plane[:, b, m0:m1], woven[:])

        for i in range(BLOCKS * PACK):
            first_stage(i)
            if i >= 1:
                pick_a(i - 1, i == BLOCKS * PACK - 1)
                if i - 1 < PACK:
                    pick_b(i - 1, 0, PAIRS, False)
            if i == 1:
                prepare_second_block()
                wo_codes = held.tile([P, BLOCKS, N], U16, name="wo_codes", tag="words_raw", align_bytes=64)
                nc.sync.dma_start(out=wo_codes[:].bitcast(I32), in_=wo_words.rearrange("a p c -> p a c").bitcast(I32))
                wo_plane = held.tile([P, BLOCKS, N], U8, name="wo_plane", tag="planes_raw", align_bytes=64)
                nc.gpsimd.memset(wo_plane[:].rearrange("p a n -> p (a n)").bitcast(I32), 0)
                load_scale_rows(
                    nc.sync, wo_plane[:].bitcast(I32), 0,
                    lambda r: wo_scales[:, r:16:4, :].rearrange("a q n -> q a n").bitcast(I32),
                )
            if i in (2, 3):
                prepare_wt(i - 2)
            if i in (PACK, PACK + 1):
                rows, codes, plane = ((xa_rows, xa_codes, xa_plane), (xb_rows, xb_codes, xb_plane))[i - PACK]
                weave_and_quantize(nc.scalar.copy, rows, codes, plane, 0, 0, PAIRS)
        emph_sb = held.tile([P, N // P, PAIRS], F32, name="emph_sb", tag="rows_raw", align_bytes=64)
        nc.sync.dma_start(out=emph_sb[:], in_=emph.rearrange("(u p) m -> p u m", p=P))

        last = BLOCKS - 1
        tiles_n = N // P
        chunks = ((0, 256), (256, 384), (384, 512))
        sums = {}
        opens = {}
        closes = {}
        spare_tags = [("e2", 2), ("e2", 2), ("e1", 3), ("e3", 3)]
        for c, (m0, m1) in enumerate(chunks):
            per_bank = BANK // (m1 - m0)
            for u0 in range(0, tiles_n, per_bank):
                tag, bufs = spare_tags.pop(0)
                bank = psum.tile([P, per_bank, m1 - m0], F32, name="sum", tag=tag, bufs=bufs)
                for u in range(u0, u0 + per_bank):
                    sums[c, u] = bank
                    opens[c, u] = u == u0
                    closes[c, u] = u == u0 + per_bank - 1

        def second_stage(c, b, use_xa):
            m0, m1 = chunks[c]
            per_bank = BANK // (m1 - m0)
            for u in range(tiles_n):
                cols = slice(u * P, (u + 1) * P)
                if use_xa:
                    nc.tensor.matmul_mx(
                        out=sums[c, u][:, u % per_bank, :], lhsT=wt_codes[:, b, cols].bitcast(FP8X4), lhsT_scale=wt_plane[:, b, cols],
                        rhs=xa_codes[:, b, m0:m1].bitcast(FP8X4), rhs_scale=xa_plane[:, b, m0:m1],
                        start=(b == 0 and opens[c, u]), stop=False,
                    )
                else:
                    nc.tensor.matmul_mx(
                        out=sums[c, u][:, u % per_bank, :], lhsT=wo_codes[:, b, cols].bitcast(FP4X4), lhsT_scale=wo_plane[:, b, cols],
                        rhs=xb_codes[:, b, m0:m1].bitcast(FP8X4), rhs_scale=xb_plane[:, b, m0:m1],
                        start=False, stop=(b == last and closes[c, u]),
                    )

        def finish(c):
            m0, m1 = chunks[c]
            per_bank = BANK // (m1 - m0)
            for u0 in range(0, tiles_n, per_bank):
                scores = held.tile([P, per_bank, m1 - m0], F32, name=f"scores{c}_{u0}", align_bytes=64)
                nc.vector.tensor_tensor(scores[:], sums[c, u0][:], emph_sb[:, u0 : u0 + per_bank, m0:m1], ALU.mult)
                nc.sync.dma_start(
                    out=out[u0 * P : (u0 + per_bank) * P, m0:m1].rearrange("(u p) m -> p u m", p=P), in_=scores[:]
                )

        for c in range(len(chunks)):
            second_stage(c, 0, True)
            second_stage(c, 0, False)
        pick_a(BLOCKS * PACK - 1, True)
        weave_and_quantize(nc.scalar.copy, xa_rows, xa_codes, xa_plane, last, 0, PAIRS)
        for c in range(len(chunks)):
            second_stage(c, last, True)
        for c, (m0, m1) in enumerate(chunks):
            for t in range(PACK):
                pick_b(last * PACK + t, m0, m1, True)
            weave_and_quantize(nc.scalar.copy, xb_rows, xb_codes, xb_plane, last, m0, m1)
            second_stage(c, last, False)
        for c in range(len(chunks)):
            finish(c)
